import numpy as np
import ml_dtypes


def mxq(x, axis, fmt="e4m3"):
    dtype, down = {"e4m3": (ml_dtypes.float8_e4m3fn, 7), "e5m2": (ml_dtypes.float8_e5m2, 14)}[fmt]
    v = np.moveaxis(np.asarray(x, np.float32).astype(ml_dtypes.bfloat16).astype(np.float64), axis, -1)
    blocks = v.reshape(v.shape[:-1] + (-1, 32))
    amax = np.abs(blocks).max(-1, keepdims=True)
    byte = np.maximum(np.where(amax > 0, np.frexp(amax)[1] - 1 + 127, 0) - down, 1)
    scale = np.exp2(byte - 127.0)
    codes = (blocks / scale).astype(np.float32).astype(dtype).astype(np.float64)
    return np.moveaxis((codes * scale).reshape(v.shape), -1, axis)


WIDE = False


def mx_kscale(k):
    if not WIDE:
        return np.ones(k)
    levels = np.array([10, -10, 5, -5, 0])
    if k % 512:
        return np.exp2(np.random.permutation(np.resize(levels, k // 32))).repeat(32)
    a = np.empty((k // 512, 16))
    for p in range(k // 512):
        a[p, :8] = np.random.permutation(np.resize(levels, 8))
        for g in range(8):
            far = levels[np.abs(levels - a[p, g]) >= 10]
            a[p, g + 8] = far[np.random.randint(len(far))]
    return np.exp2(a.ravel()).repeat(32)


BF16 = ml_dtypes.bfloat16


def bf(x):
    return np.asarray(x, np.float32).astype(BF16)


def f64(x):
    return np.asarray(x).astype(np.float64)


E2M1 = np.array([0.0, 0.5, 1.0, 1.5, 2.0, 3.0, 4.0, 6.0, -0.0, -0.5, -1.0, -1.5, -2.0, -3.0, -4.0, -6.0])


def pack_weight(w, fmt):
    k, n = w.shape
    w = f64(bf(w)).reshape(k // 32, 32, n)
    amax = np.abs(w).max(1)
    if fmt == "e4m3":
        byte = np.frexp(amax)[1] - 1 + 127 - 7
    else:
        mant, ex = np.frexp(amax / 6.0)
        byte = np.where(mant > 0.5, ex, ex - 1) + 127
    byte = np.clip(np.where(amax > 0, byte, 1), 1, 254)
    scaled = (w * np.exp2(127.0 - byte)[:, None, :]).reshape(k, n).astype(np.float32)
    by_word = np.ascontiguousarray(scaled.reshape(k // 512, 128, 4, n).transpose(0, 1, 3, 2))
    if fmt == "e4m3":
        words = by_word.astype(ml_dtypes.float8_e4m3fn).view(np.uint8)
    else:
        c = by_word.astype(ml_dtypes.float4_e2m1fn).view(np.uint8) & 0xF
        words = c[..., 0::2] | (c[..., 1::2] << 4)
    return np.ascontiguousarray(words), np.ascontiguousarray(byte.astype(np.uint8).reshape(k // 512, 16, n))


def unpack_weight(words, scales, fmt):
    g, p, n, _ = words.shape
    if fmt == "e4m3":
        vals = np.ascontiguousarray(words).view(ml_dtypes.float8_e4m3fn).astype(np.float64)
    else:
        nib = np.empty((g, p, n, 4), np.uint8)
        nib[..., 0::2] = words & 0xF
        nib[..., 1::2] = words >> 4
        vals = E2M1[nib]
    vals = vals * np.repeat(np.exp2(scales.astype(np.float64) - 127.0), 8, axis=1)[..., None]
    return vals.transpose(0, 1, 3, 2).reshape(g * 512, n)
def pack4(w):
    words, scales = pack_weight(w, "e2m1")
    return words.reshape(words.shape[0], 128, -1), scales


def unpack4(words, scales):
    return unpack_weight(words.reshape(words.shape[0], 128, -1, 2), scales, "e2m1")


def planes(Y):
    n, m = Y.shape
    b = f64(bf(Y)).reshape(n // 32, 32, m)
    amax = np.abs(b).max(1)
    byte = np.clip(np.where(amax > 0, np.frexp(amax)[1] - 1 + 127 - 7, 1), 1, 254)
    codes = (b * np.exp2(127.0 - byte)[:, None, :]).reshape(n, m).astype(np.float32).astype(ml_dtypes.float8_e4m3fn).view(np.uint8)
    words = codes.reshape(n // 512, 128, 4, m).transpose(0, 1, 3, 2)
    return np.ascontiguousarray(words), np.ascontiguousarray(byte.astype(np.uint8).reshape(n // 512, 16, m))


T, D = 1024, 1536


def setup_inputs():
    se = mx_kscale(D)
    sh = mx_kscale(D)
    spread = np.exp(0.6 * np.random.randn(D))
    xe = np.random.randn(D, T) * se[:, None]
    xh = np.random.randn(D, T) * sh[:, None]
    emb_words, emb_scales = pack_weight(xe, "e4m3")
    hid_words, hid_scales = pack_weight(xh, "e4m3")
    w_emb = bf(np.random.randn(D, D) / np.sqrt(2 * D) * spread / se[:, None])
    w_hid = bf(np.random.randn(D, D) / np.sqrt(2 * D) * spread / sh[:, None])
    bias = bf(0.4 * np.random.randn(D) * spread)
    return {"emb_words": emb_words, "emb_scales": emb_scales,
            "hid_words": hid_words, "hid_scales": hid_scales,
            "w_emb": w_emb, "w_hid": w_hid, "bias": bias}


def reference(emb_words, emb_scales, hid_words, hid_scales, w_emb, w_hid, bias):
    xe = unpack_weight(emb_words, emb_scales, "e4m3")
    xh = unpack_weight(hid_words, hid_scales, "e4m3")
    pe = xe.T @ mxq(f64(w_emb), 0, "e4m3")
    ph = xh.T @ mxq(f64(w_hid), 0, "e4m3")
    y = pe + ph + f64(bias)
    Y = y.T
    words, scales = planes(Y)
    return y, words, scales

@@ -1,0 +1,339 @@
+from contextlib import ExitStack
+
+import concourse.mybir as mybir
+from concourse.masks import make_identity
+
+T, D = 1024, 1536
+FLOPS = 2 * T * 2 * D * D
+
+F32 = mybir.dt.float32
+BF16 = mybir.dt.bfloat16
+I32 = mybir.dt.int32
+U32 = mybir.dt.uint32
+U8 = mybir.dt.uint8
+FP8X4 = mybir.dt.float8_e4m3fn_x4
+ADD = mybir.AluOpType.add
+
+P = 128
+K_PASS = 512
+N_TILE = 512
+PASSES = 6
+SWEEPS = 3
+TOKEN_TILES = 8
+HALF = N_TILE // 2
+EARLY_VECTOR_COLS = 336
+
+
+def vector_cols(g, n):
+    return EARLY_VECTOR_COLS if n == 0 or (g, n) == (0, 1) else HALF
+
+
+def tensor_order():
+    order = [("bias_turn",)]
+    order += [("mm", 0, t, g, t) for g in range(PASSES) for t in range(TOKEN_TILES)]
+    wave = sorted((g + t // 4, t, g) for t in range(TOKEN_TILES) for g in range(PASSES))
+    order += [("mm", 1, t, g, t) for step, t, g in wave]
+    turn_steps = [0, 3, 5, 7]
+    for step in range(PASSES + 2):
+        if step in turn_steps:
+            n, first = divmod(4 * turn_steps.index(step), TOKEN_TILES)
+            order += [("turn", n, first, 2, 0), ("turn", n, first + 2, 2, 1)]
+        order += [("mm", 2, t, step - t // 2, 2 + t) for t in range(6) if 0 <= step - t // 2 < PASSES]
+    order += [("mm", 2, 6, g, 2) for g in range(PASSES)]
+    order += [("turn", 2, 0, 2, 0), ("turn", 2, 2, 2, 1)]
+    order += [("mm", 2, 7, g, 3) for g in range(PASSES)]
+    order += [("turn", 2, 4, 2, 4), ("turn", 2, 6, 1, 5), ("turn", 2, 7, 1, 6)]
+    return order
+
+
+VECTOR_TEXT = """
+b00 q00 h b10 q10 b20 q20 b30 q30 b40 q40 b50 q50 b01 q01
+e00 b11 e01 e02 e03 q11 e04 e05 e06 e07
+q21 b41 q31 b51 q41 b02 q51 b12 q02 b22 q12 b32 q22
+e10 e11 e12 e13 e14 e15 q32 b42 e16 z00 e17 z02 q42 b52 q52 z04 z06
+e20 z10 z12 e21 e22 e23 e24 e25 z14 z16 e26 c26 z20 z22 c27 e27 z24 z26 z27
+"""
+SCALAR_TEXT = """
+a00 B a10 a20 a30 a40 a50 a01
+a11 a21 b21 a31 b31 a41 a51 a02 a12 a22 c00 c01 c02 c03 a32 a42 c04 c05
+y00 y02 c06 c07 a52 c10 c11 y04 y06 c12 c13 c14 c15 c16 c17 y10 y12
+c20 c21 c22 c23 y14 y16 c24 c25 y20 y22 y24 y26 y27 s232 s233
+"""
+STORE_TEXT = """
+o002 o022 o042 o062 o102 o122 o142 w004 o162 w044 o201 w104 o211 o221 o231 o241 o251 w144
+s020 s021 s022 s023 o261 w204 o271 w242 w262 s230 s231
+"""
+KINDS = {"a": "mix_a", "b": "mix_b", "q": "quant_w", "e": "drain", "c": "cast", "y": "gather", "z": "quant_y",
+         "o": "store_y", "w": "store_words", "s": "store_scales", "h": "hid_memset", "B": "bias_copy"}
+
+
+def parse(text):
+    return [(KINDS[word[0]],) + tuple(int(c) for c in word[1:]) for word in text.split()]
+
+
+def load_order():
+    order = []
+    for g in range(PASSES - 1):
+        order += [("load_w", g, 0), ("load_x", g)]
+    order += [("load_w", 5, 0), ("load_w", 0, 1), ("load_x", 5)]
+    order += [("load_w", g, 1) for g in range(1, PASSES)] + [("load_w", g, 2) for g in range(PASSES)]
+    return order
+
+
+def queues():
+    return {
+        "tensor": tensor_order(),
+        "vector": [("emb_memset",)] + parse(VECTOR_TEXT),
+        "scalar": [("load_bias",)] + parse(SCALAR_TEXT),
+        "sync": load_order() + parse(STORE_TEXT),
+        "gpsimd": [("identity",), ("load_scales", 0), ("load_scales", 1)],
+    }
+
+
+def needs(step, bank_reader, turn_of):
+    kind = step[0]
+    if kind == "mm":
+        n, t, g, bank = step[1:]
+        out = [("quant_w", g, n), ("load_x", g), ("load_scales", g // 3)]
+        return out + bank_reader.get(step, [])
+    if kind == "turn":
+        n, t, count, bank = step[1:]
+        return [("cast", n, t + i) for i in range(count)] + bank_reader.get(step, [])
+    if kind in ("mix_a", "mix_b"):
+        return [("load_w",) + step[1:]]
+    if kind == "quant_w":
+        return [("mix_a",) + step[1:], ("mix_b",) + step[1:]]
+    if kind == "drain":
+        return [turn_of["close", step[1], step[2]], ("bias_copy",)]
+    if kind == "cast":
+        if step[1:] == (2, 7):
+            return [turn_of["close", 2, 7]]
+        return [("drain",) + step[1:]]
+    if kind == "gather":
+        return [turn_of["turn", step[1], step[2]]]
+    if kind == "quant_y":
+        return [("gather",) + step[1:]]
+    if kind == "store_y":
+        return [("drain", step[1], step[2] + i) for i in range(step[3])]
+    if kind == "store_words":
+        return [("quant_y", step[1], t) for t in range(step[2], step[2] + step[3]) if ("turn", step[1], t) in turn_of]
+    if kind == "store_scales":
+        return [("quant_y", n, t) for n in range(step[1], step[2]) for t in range(TOKEN_TILES) if ("turn", n, t) in turn_of]
+    if kind == "load_scales":
+        return [("emb_memset",)] if step[1] == 0 else [("hid_memset",)]
+    if kind == "bias_turn":
+        return [("identity",), ("load_bias",)]
+    if kind == "bias_copy":
+        return [("bias_turn",)]
+    return []
+
+
+def program():
+    lists = queues()
+    bank_reader, turn_of = {}, {}
+    last = {6: [("bias_copy",)], 7: [("bias_copy",)]}
+    for step in lists["tensor"]:
+        if step[0] == "mm":
+            n, t, g, bank = step[1:]
+            if g == 0:
+                bank_reader[step] = last.get(bank, [])
+                last[bank] = [("drain", n, t)]
+            if g == PASSES - 1:
+                turn_of["close", n, t] = step
+        if step[0] == "turn":
+            n, t, count, bank = step[1:]
+            bank_reader[step] = last.get(bank, [])
+            last[bank] = [("gather", n, t)]
+            turn_of["turn", n, t] = step
+    text, written = [], set()
+    place = {engine: 0 for engine in lists}
+    total = sum(len(steps) for steps in lists.values())
+    while len(text) < total:
+        before = len(text)
+        for engine, steps in lists.items():
+            if place[engine] < len(steps):
+                step = steps[place[engine]]
+                wanted = needs(step, bank_reader, turn_of)
+                if all(w in written for w in wanted):
+                    text.append((engine, step, wanted))
+                    written.add(step)
+                    place[engine] += 1
+        assert len(text) > before
+    return text, turn_of
+
+
+def tile_mtp_combined_projection_g6_kernel(
+    tc, emb_words, emb_scales, hid_words, hid_scales, w_emb, w_hid, bias, out_0, out_1, out_2
+):
+    nc = tc.nc
+    engines = {"vector": nc.vector, "scalar": nc.scalar, "sync": nc.sync}
+    weights = (w_emb, w_hid)
+    x_words = (emb_words, hid_words)
+    x_scale_rows = (emb_scales, hid_scales)
+
+    with ExitStack() as ctx:
+        keep = ctx.enter_context(tc.tile_pool(name="keep", bufs=1))
+        stage = ctx.enter_context(tc.tile_pool(name="stage", bufs=1))
+        psum = ctx.enter_context(tc.psum_pool(name="psum", bufs=1))
+        ctx.enter_context(tc.manual_schedule())
+
+        identity = keep.tile([P, P], F32)
+        bias_quads = keep.tile([P, SWEEPS, 4], BF16)
+        bias_rows = keep.tile([P, D], BF16)
+        x_codes = keep.tile([P, PASSES, T], U32, align_bytes=64)
+        emb_planes = keep.tile([P, T], U8, align_bytes=64)
+        hid_planes = keep.tile([P, T], U8, align_bytes=64)
+        x_planes = (emb_planes, hid_planes)
+        w_codes = keep.tile([P, SWEEPS, PASSES, N_TILE], U32, align_bytes=64)
+        w_scales = keep.tile([P, SWEEPS, PASSES, N_TILE], U8, align_bytes=64)
+        y_f32 = keep.tile([P, SWEEPS, TOKEN_TILES, N_TILE], F32)
+        y_bf16 = keep.tile([P, SWEEPS, TOKEN_TILES, N_TILE], BF16)
+        y_codes = keep.tile([P, SWEEPS, T], U32, align_bytes=64)
+        y_scales = keep.tile([P, SWEEPS, T], U8, align_bytes=64)
+
+        raw, grouped, banks, turned = {}, {}, {}, {}
+
+        def copy(engine, out, in_):
+            if engine == "vector":
+                nc.vector.tensor_copy(out=out, in_=in_)
+            else:
+                nc.scalar.copy(out=out, in_=in_)
+
+        def bank_tile(bank):
+            return psum.tile([P, N_TILE], F32, name="bank%d" % bank)
+
+        def word_order(ap):
+            return ap.rearrange("p (q u e) -> p u q e", u=2, e=2)
+
+        text, turn_of = program()
+        for engine, step, wanted in text:
+            kind = step[0]
+            if kind == "identity":
+                make_identity(nc, identity[:])
+            elif kind == "load_bias":
+                nc.scalar.dma_start(out=bias_quads[:], in_=bias.rearrange("(n p c) -> p n c", n=SWEEPS, c=4))
+            elif kind == "bias_turn":
+                words = bias_quads[:].rearrange("p n c -> p (n c)").bitcast(F32)
+                banks["bias"] = (bank_tile(6), bank_tile(7))
+                for j in range(2 * SWEEPS):
+                    nc.tensor.transpose(
+                        banks["bias"][j // 4][:, (j % 4) * P : (j % 4 + 1) * P],
+                        words[:, j : j + 1].to_broadcast([P, P]),
+                        identity[:],
+                    )
+            elif kind == "bias_copy":
+                for n in range(SWEEPS):
+                    src = banks["bias"][n // 2][:, (n % 2) * 2 * P : (n % 2 + 1) * 2 * P]
+                    dst = bias_rows[:, n * N_TILE : (n + 1) * N_TILE].bitcast(F32)
+                    nc.scalar.copy(out=dst.rearrange("p (q u) -> p q u", u=2), in_=src.rearrange("p (u q) -> p q u", u=2))
+            elif kind in ("emb_memset", "hid_memset"):
+                nc.vector.memset(x_planes[kind == "hid_memset"][:].bitcast(I32), 0)
+            elif kind == "load_scales":
+                side = step[1]
+                for quad in range(4):
+                    nc.gpsimd.dma_start(
+                        out=x_planes[side][32 * quad : 32 * quad + 12, :].bitcast(I32),
+                        in_=x_scale_rows[side][:, 4 * quad : 4 * quad + 4, :].bitcast(I32),
+                    )
+            elif kind == "load_x":
+                side, group = divmod(step[1], 3)
+                nc.sync.dma_start(
+                    out=x_codes[:, step[1], :].bitcast(I32),
+                    in_=x_words[side][group].rearrange("p m t -> p (m t)").bitcast(I32),
+                )
+            elif kind == "load_w":
+                g, n = step[1:]
+                side, group = divmod(g, 3)
+                raw[g, n] = stage.tile([P, 4, N_TILE], BF16, name="raw", bufs=6)
+                rows = weights[side][group * K_PASS : (group + 1) * K_PASS, n * N_TILE : (n + 1) * N_TILE]
+                nc.sync.dma_start(out=raw[g, n][:], in_=rows.rearrange("(p j) c -> p j c", j=4))
+            elif kind in ("mix_a", "mix_b"):
+                g, n = step[1:]
+                if (g, n) not in grouped:
+                    grouped[g, n] = stage.tile([P, N_TILE, 4], BF16, name="grouped", bufs=5, align_bytes=64)
+                split = vector_cols(g, n)
+                cols = slice(0, split) if kind == "mix_b" else slice(split, N_TILE)
+                copy(
+                    engine,
+                    grouped[g, n][:, cols, :].rearrange("p (c i) j -> p c j i", i=4),
+                    raw[g, n][:, :, cols].rearrange("p j (c i) -> p c j i", i=4),
+                )
+            elif kind == "quant_w":
+                g, n = step[1:]
+                nc.vector.quantize_mx(
+                    out=w_codes[:, n, g, :].bitcast(FP8X4),
+                    scales=w_scales[:, n, g, :],
+                    in_=grouped[g, n][:].rearrange("p c j -> p (c j)"),
+                )
+            elif kind == "mm":
+                n, t, g, bank = step[1:]
+                if g == 0:
+                    banks[n, t] = bank_tile(bank)
+                side, group = divmod(g, 3)
+                tokens = slice(t * P, (t + 1) * P)
+                nc.tensor.matmul_mx(
+                    out=banks[n, t][:],
+                    lhsT=x_codes[:, g, tokens].bitcast(FP8X4),
+                    lhsT_scale=x_planes[side][4 * group :, tokens],
+                    rhs=w_codes[:, n, g, :].bitcast(FP8X4),
+                    rhs_scale=w_scales[:, n, g, :],
+                    start=(g == 0),
+                    stop=(g == PASSES - 1),
+                )
+            elif kind == "drain":
+                n, t = step[1:]
+                nc.vector.tensor_tensor(
+                    out=y_f32[:, n, t, :], in0=banks[n, t][:], in1=bias_rows[:, n * N_TILE : (n + 1) * N_TILE], op=ADD
+                )
+            elif kind == "cast":
+                n, t = step[1:]
+                dst = y_bf16[:, n, t, :].rearrange("p (u q e) -> p u q e", u=2, e=2)
+                if (n, t) == (2, 7):
+                    nc.vector.tensor_tensor(
+                        out=dst,
+                        in0=word_order(banks[n, t][:]),
+                        in1=word_order(bias_rows[:, n * N_TILE : (n + 1) * N_TILE]),
+                        op=ADD,
+                    )
+                else:
+                    copy(engine, dst, word_order(y_f32[:, n, t, :]))
+            elif kind == "turn":
+                n, t, count, bank = step[1:]
+                banks["turn", n, t] = bank_tile(bank)
+                for i in range(count):
+                    words = y_bf16[:, n, t + i, :].bitcast(F32)
+                    for u in range(2):
+                        col = (2 * i + u) * P
+                        nc.tensor.transpose(banks["turn", n, t][:, col : col + P], words[:, u * P : (u + 1) * P], identity[:])
+            elif kind == "gather":
+                n, t = step[1:]
+                count = turn_of["turn", n, t][3]
+                turned[n, t] = stage.tile([P, 2 * P * 4], BF16, name="turned", bufs=4, align_bytes=64)
+                nc.scalar.copy(
+                    out=turned[n, t][:, : count * 4 * P].bitcast(F32).rearrange("p (i m u) -> p i m u", i=count, u=2),
+                    in_=banks["turn", n, t][:, : count * 2 * P].rearrange("p (i u m) -> p i m u", i=count, u=2),
+                )
+            elif kind == "quant_y":
+                n, t = step[1:]
+                count = turn_of["turn", n, t][3]
+                tokens = slice(t * P, (t + count) * P)
+                nc.vector.quantize_mx(
+                    out=y_codes[:, n, tokens].bitcast(FP8X4),
+                    scales=y_scales[:, n, tokens],
+                    in_=turned[n, t][:, : count * 4 * P],
+                )
+            elif kind == "store_y":
+                n, t, count = step[1:]
+                rows = out_0[t * P : (t + count) * P, n * N_TILE : (n + 1) * N_TILE]
+                nc.sync.dma_start(out=rows.rearrange("(i p) f -> p i f", p=P), in_=y_f32[:, n, t : t + count, :])
+            elif kind == "store_words":
+                n, t, count = step[1:]
+                words = out_1[n].rearrange("p m t -> p (m t)").bitcast(I32)
+                tokens = slice(t * P, (t + count) * P)
+                nc.sync.dma_start(out=words[:, tokens], in_=y_codes[:, n, tokens].bitcast(I32))
+            elif kind == "store_scales":
+                first, end, quad = step[1:]
+                rows = out_2[first:end, 4 * quad : 4 * quad + 4, :].rearrange("n r m -> r n m")
+                engines[engine].dma_start(
+                    out=rows.bitcast(I32), in_=y_scales[32 * quad : 32 * quad + 4, first:end, :].bitcast(I32)
+                )

@@ -47,7 +47,7 @@ def tensor_order():
 
 
 VECTOR_TEXT = """
-b00 q00 h b10 q10 b20 q20 b30 q30 b40 q40 b50 q50 b01 q01
+h b00 q00 b10 q10 b20 q20 b30 q30 b40 q40 b50 q50 b01 q01
 e00 b11 e01 e02 e03 q11 e04 e05 e06 e07
 q21 b41 q31 b51 q41 b02 q51 b12 q02 b22 q12 b32 q22
 e10 e11 e12 e13 e14 e15 q32 b42 e16 z00 e17 z02 q42 b52 q52 z04 z06
@@ -75,6 +75,10 @@ def load_order():
     order = []
     for g in range(PASSES - 1):
         order += [("load_w", g, 0), ("load_x", g)]
+        if g == 0:
+            order += [("load_scales", 0, 2), ("load_scales", 0, 3)]
+        if g == 2:
+            order += [("load_scales", 1, quad) for quad in range(4)]
     order += [("load_w", 5, 0), ("load_w", 0, 1), ("load_x", 5)]
     order += [("load_w", g, 1) for g in range(1, PASSES)] + [("load_w", g, 2) for g in range(PASSES)]
     return order
@@ -84,9 +88,9 @@ def queues():
     return {
         "tensor": tensor_order(),
         "vector": [("emb_memset",)] + parse(VECTOR_TEXT),
-        "scalar": [("load_bias",)] + parse(SCALAR_TEXT),
+        "scalar": [("load_bias",), ("load_scales", 0, 0), ("load_scales", 0, 1)] + parse(SCALAR_TEXT),
         "sync": load_order() + parse(STORE_TEXT),
-        "gpsimd": [("identity",), ("load_scales", 0), ("load_scales", 1)],
+        "gpsimd": [("identity",)],
     }
 
 
@@ -94,7 +98,7 @@ def needs(step, bank_reader, turn_of):
     kind = step[0]
     if kind == "mm":
         n, t, g, bank = step[1:]
-        out = [("quant_w", g, n), ("load_x", g), ("load_scales", g // 3)]
+        out = [("quant_w", g, n), ("load_x", g)] + [("load_scales", g // 3, quad) for quad in range(4)]
         return out + bank_reader.get(step, [])
     if kind == "turn":
         n, t, count, bank = step[1:]
@@ -229,12 +233,11 @@ def tile_mtp_combined_projection_g6_kernel(
             elif kind in ("emb_memset", "hid_memset"):
                 nc.vector.memset(x_planes[kind == "hid_memset"][:].bitcast(I32), 0)
             elif kind == "load_scales":
-                side = step[1]
-                for quad in range(4):
-                    nc.gpsimd.dma_start(
-                        out=x_planes[side][32 * quad : 32 * quad + 12, :].bitcast(I32),
-                        in_=x_scale_rows[side][:, 4 * quad : 4 * quad + 4, :].bitcast(I32),
-                    )
+                side, quad = step[1:]
+                engines[engine].dma_start(
+                    out=x_planes[side][32 * quad : 32 * quad + 12, :].bitcast(I32),
+                    in_=x_scale_rows[side][:, 4 * quad : 4 * quad + 4, :].bitcast(I32),
+                )
             elif kind == "load_x":
                 side, group = divmod(step[1], 3)
                 nc.sync.dma_start(

@@ -22,46 +22,45 @@ SWEEPS = 3
 TOKEN_TILES = 8
 HALF = N_TILE // 2
 EARLY_VECTOR_COLS = 336
+TURN_AFTER = [4, 6, 8, 9, 13]
+SHARES = {(5, 0): 256, (5, 1): 256}
 
 
 def vector_cols(g, n):
-    return EARLY_VECTOR_COLS if n == 0 or (g, n) == (0, 1) else HALF
+    if (g, n) in SHARES:
+        return SHARES[g, n]
+    if n == 0 or (g, n) == (5, 1):
+        return EARLY_VECTOR_COLS
+    return 256 if n == 1 else HALF
 
 
 def tensor_order():
     order = [("bias_turn",)]
-    order += [("mm", 0, t, g, t) for g in range(PASSES) for t in range(TOKEN_TILES)]
-    wave = sorted((g + t // 4, t, g) for t in range(TOKEN_TILES) for g in range(PASSES))
-    order += [("mm", 1, t, g, t) for step, t, g in wave]
-    turn_steps = [0, 3, 5, 7]
-    for step in range(PASSES + 2):
-        if step in turn_steps:
-            n, first = divmod(4 * turn_steps.index(step), TOKEN_TILES)
-            order += [("turn", n, first, 2, 0), ("turn", n, first + 2, 2, 1)]
-        order += [("mm", 2, t, step - t // 2, 2 + t) for t in range(6) if 0 <= step - t // 2 < PASSES]
-    order += [("mm", 2, 6, g, 2) for g in range(PASSES)]
-    order += [("turn", 2, 0, 2, 0), ("turn", 2, 2, 2, 1)]
-    order += [("mm", 2, 7, g, 3) for g in range(PASSES)]
-    order += [("turn", 2, 4, 2, 4), ("turn", 2, 6, 1, 5), ("turn", 2, 7, 1, 6)]
+    order += [("mm", n, t, g, 4 * n + t) for g in range(PASSES) for n in range(2) for t in range(4)]
+    tiles = [(n, t) for t in range(4, 8) for n in range(2)] + [(2, t) for t in range(TOKEN_TILES)]
+    after = TURN_AFTER
+    runs = [[(0, 0), (0, 1)], [(0, 2), (0, 3)], [(0, 4), (0, 5)], [(0, 6), (0, 7)], [(2, 0), (2, 2)]]
+    for j, (n, t) in enumerate(tiles):
+        order += [("mm", n, t, g, j % 4) for g in range(PASSES)]
+        if j in after:
+            r = after.index(j)
+            order += [("turn",) + unit + (2, 4 + 2 * (r % 2) + i) for i, unit in enumerate(runs[r])]
+    order += [("turn", 2, 4, 2, 6), ("turn", 2, 6, 1, 7), ("turn", 2, 7, 1, 4)]
     return order
 
 
 VECTOR_TEXT = """
-h b00 q00 b10 q10 b20 q20 b30 q30 b40 q40 b50 q50 b01 q01
-e00 b11 e01 e02 e03 q11 e04 e05 e06 e07
-q21 b41 q31 b51 q41 b02 q51 b12 q02 b22 q12 b32 q22
-e10 e11 e12 e13 e14 e15 q32 b42 e16 z00 e17 z02 q42 b52 q52 z04 z06
-e20 z10 z12 e21 e22 e23 e24 e25 z14 z16 e26 c26 z20 z22 c27 e27 z24 z26 z27
+b00 b01 q00 q01 b10 b11 q10 q11 b20 b21 q20 q21 b30 b31 q30 q31 b40 b41 q40 b50 q41 q50 b51 q51
+e00 e01 e10 e11 e02 e12 e03 e13
+e04 b02 e14 q02 b12 e05 q12 b22 e15 q22 b32 e06 q32 b42 z00 z10 e16 q42 b52 e07 q52 c05 e17 z02 z12
+e20 z04 z14 e21 z06 z16 e22 e23 e24 e25 c24 z20 e26 c26 c27 e27 z24 z26 z27
 """
 SCALAR_TEXT = """
-a00 B a10 a20 a30 a40 a50 a01
-a11 a21 b21 a31 b31 a41 a51 a02 a12 a22 c00 c01 c02 c03 a32 a42 c04 c05
-y00 y02 c06 c07 a52 c10 c11 y04 y06 c12 c13 c14 c15 c16 c17 y10 y12
-c20 c21 c22 c23 y14 y16 c24 c25 y20 y22 y24 y26 y27 s232 s233
+B a00 a01 a10 a11 a20 a21 a30 a31 a40 a41 a50 a51
+c00 c01 a02 a12 a22 c02 a32 y00 y01 a42 c03 a52 y02 y03 c04 c06 c07 y04 y05 y06 y07 c20 c22 y20 y22 y24 y26 y27 s23082 s23083
 """
 STORE_TEXT = """
-o002 o022 o042 o062 o102 o122 o142 w004 o162 w044 o201 w104 o211 o221 o231 o241 o251 w144
-s020 s021 s022 s023 o261 w204 o271 w242 w262 s230 s231
+o00 o01 o02 o03 o04 o05 o06 w004 w104 o07 o20 o21 w044 w144 s02080 s02081 s02082 s02083 o22 o23 o24 o25 w204 o26 o27 w242 w262 s23080 s23081
 """
 KINDS = {"a": "mix_a", "b": "mix_b", "q": "quant_w", "e": "drain", "c": "cast", "y": "gather", "z": "quant_y",
          "o": "store_y", "w": "store_words", "s": "store_scales", "h": "hid_memset", "B": "bias_copy"}
@@ -74,55 +73,68 @@ def parse(text):
 def load_order():
     order = []
     for g in range(PASSES - 1):
-        order += [("load_w", g, 0), ("load_x", g)]
-        if g == 0:
-            order += [("load_scales", 0, 2), ("load_scales", 0, 3)]
-        if g == 2:
-            order += [("load_scales", 1, quad) for quad in range(4)]
-    order += [("load_w", 5, 0), ("load_w", 0, 1), ("load_x", 5)]
-    order += [("load_w", g, 1) for g in range(1, PASSES)] + [("load_w", g, 2) for g in range(PASSES)]
+        order += [("load_w", g, 0, 2), ("load_x", g, 0)]
+    order += [("load_w", 5, 0, 1), ("load_w", 5, 1, 1), ("load_x", 5, 0)]
+    order += [("load_x", g, 1) for g in range(PASSES)] + [("load_w", g, 2, 1) for g in range(PASSES)]
     return order
 
 
 def queues():
     return {
         "tensor": tensor_order(),
-        "vector": [("emb_memset",)] + parse(VECTOR_TEXT),
-        "scalar": [("load_bias",), ("load_scales", 0, 0), ("load_scales", 0, 1)] + parse(SCALAR_TEXT),
+        "vector": [("emb_memset",), ("hid_memset",)] + parse(VECTOR_TEXT),
+        "scalar": [("load_bias",)] + [("load_scales", 0, quad) for quad in range(4)] + parse(SCALAR_TEXT),
         "sync": load_order() + parse(STORE_TEXT),
-        "gpsimd": [("identity",)],
+        "gpsimd": [("identity",)] + [("load_scales", 1, quad) for quad in range(4)],
     }
+
+
+def quant_tokens(n, t):
+    return {(2, 0): 4, (2, 6): 1, (2, 7): 1}.get((n, t), 2)
+
+
+def quant_starts(n):
+    return (0, 4, 6, 7) if n == 2 else (0, 2, 4, 6)
 
 
 def needs(step, bank_reader, turn_of):
     kind = step[0]
     if kind == "mm":
         n, t, g, bank = step[1:]
-        out = [("quant_w", g, n), ("load_x", g)] + [("load_scales", g // 3, quad) for quad in range(4)]
+        out = [("quant_w", g, n), ("load_x", g, t // 4)] + [("load_scales", g // 3, quad) for quad in range(4)]
         return out + bank_reader.get(step, [])
     if kind == "turn":
-        n, t, count, bank = step[1:]
-        return [("cast", n, t + i) for i in range(count)] + bank_reader.get(step, [])
+        return [("cast", step[1], step[2])] + bank_reader.get(step, [])
     if kind in ("mix_a", "mix_b"):
-        return [("load_w",) + step[1:]]
+        g, n = step[1:]
+        return [("load_w", g, 0, 2)] if n < 2 and g < 5 else [("load_w", g, n, 1)]
     if kind == "quant_w":
         return [("mix_a",) + step[1:], ("mix_b",) + step[1:]]
     if kind == "drain":
         return [turn_of["close", step[1], step[2]], ("bias_copy",)]
     if kind == "cast":
-        if step[1:] == (2, 7):
+        n, t = step[1:]
+        if (n, t) == (2, 7):
             return [turn_of["close", 2, 7]]
-        return [("drain",) + step[1:]]
+        if n == 0:
+            return [("drain", 0, t), ("drain", 1, t)]
+        return [("drain", 2, t + i) for i in range(turn_of["turn", n, t][3])]
     if kind == "gather":
         return [turn_of["turn", step[1], step[2]]]
     if kind == "quant_y":
-        return [("gather",) + step[1:]]
+        n, t = step[1:]
+        if n < 2:
+            return [("gather", 0, t), ("gather", 0, t + 1)]
+        return [("gather", 2, 0), ("gather", 2, 2)] if t == 0 else [("gather", 2, t)]
     if kind == "store_y":
-        return [("drain", step[1], step[2] + i) for i in range(step[3])]
+        n, t = step[1:]
+        return [("drain", 0, t), ("drain", 1, t)] if n == 0 else [("drain", 2, t)]
     if kind == "store_words":
-        return [("quant_y", step[1], t) for t in range(step[2], step[2] + step[3]) if ("turn", step[1], t) in turn_of]
+        n, t, count = step[1:]
+        return [("quant_y", n, s) for s in quant_starts(n) if t <= s < t + count]
     if kind == "store_scales":
-        return [("quant_y", n, t) for n in range(step[1], step[2]) for t in range(TOKEN_TILES) if ("turn", n, t) in turn_of]
+        first, end, t, count, quad = step[1:]
+        return [("quant_y", n, s) for n in range(first, end) for s in quant_starts(n) if t <= s < t + count]
     if kind == "load_scales":
         return [("emb_memset",)] if step[1] == 0 else [("hid_memset",)]
     if kind == "bias_turn":
@@ -170,7 +182,7 @@ def tile_mtp_combined_projection_g6_kernel(
     tc, emb_words, emb_scales, hid_words, hid_scales, w_emb, w_hid, bias, out_0, out_1, out_2
 ):
     nc = tc.nc
-    engines = {"vector": nc.vector, "scalar": nc.scalar, "sync": nc.sync}
+    engines = {"scalar": nc.scalar, "sync": nc.sync, "gpsimd": nc.gpsimd}
     weights = (w_emb, w_hid)
     x_words = (emb_words, hid_words)
     x_scale_rows = (emb_scales, hid_scales)
@@ -190,12 +202,17 @@ def tile_mtp_combined_projection_g6_kernel(
         x_planes = (emb_planes, hid_planes)
         w_codes = keep.tile([P, SWEEPS, PASSES, N_TILE], U32, align_bytes=64)
         w_scales = keep.tile([P, SWEEPS, PASSES, N_TILE], U8, align_bytes=64)
-        y_f32 = keep.tile([P, SWEEPS, TOKEN_TILES, N_TILE], F32)
-        y_bf16 = keep.tile([P, SWEEPS, TOKEN_TILES, N_TILE], BF16)
+        y_wide = keep.tile([P, TOKEN_TILES, 2 * N_TILE], F32)
+        y_last = keep.tile([P, TOKEN_TILES * N_TILE], F32)
         y_codes = keep.tile([P, SWEEPS, T], U32, align_bytes=64)
         y_scales = keep.tile([P, SWEEPS, T], U8, align_bytes=64)
 
-        raw, grouped, banks, turned = {}, {}, {}, {}
+        raw, grouped, banks, rounded, turned = {}, {}, {}, {}, {}
+
+        def y_f32(n, t, count):
+            if n < 2:
+                return y_wide[:, t, n * N_TILE : (n + count) * N_TILE]
+            return y_last[:, t * N_TILE : (t + count) * N_TILE]
 
         def copy(engine, out, in_):
             if engine == "vector":
@@ -239,21 +256,26 @@ def tile_mtp_combined_projection_g6_kernel(
                     in_=x_scale_rows[side][:, 4 * quad : 4 * quad + 4, :].bitcast(I32),
                 )
             elif kind == "load_x":
-                side, group = divmod(step[1], 3)
-                nc.sync.dma_start(
-                    out=x_codes[:, step[1], :].bitcast(I32),
-                    in_=x_words[side][group].rearrange("p m t -> p (m t)").bitcast(I32),
-                )
-            elif kind == "load_w":
-                g, n = step[1:]
+                g, half = step[1:]
                 side, group = divmod(g, 3)
-                raw[g, n] = stage.tile([P, 4, N_TILE], BF16, name="raw", bufs=6)
-                rows = weights[side][group * K_PASS : (group + 1) * K_PASS, n * N_TILE : (n + 1) * N_TILE]
-                nc.sync.dma_start(out=raw[g, n][:], in_=rows.rearrange("(p j) c -> p j c", j=4))
+                tokens = slice(half * T // 2, (half + 1) * T // 2)
+                words = x_words[side][group].rearrange("p m t -> p (m t)").bitcast(I32)
+                nc.sync.dma_start(out=x_codes[:, g, tokens].bitcast(I32), in_=words[:, tokens])
+            elif kind == "load_w":
+                g, n, count = step[1:]
+                side, group = divmod(g, 3)
+                if count == 2:
+                    landed = stage.tile([P, 4, 2 * N_TILE], BF16, name="raw_wide", bufs=3)
+                else:
+                    landed = stage.tile([P, 4, N_TILE], BF16, name="raw_narrow", bufs=6)
+                for i in range(count):
+                    raw[g, n + i] = landed[:, :, i * N_TILE : (i + 1) * N_TILE]
+                rows = weights[side][group * K_PASS : (group + 1) * K_PASS, n * N_TILE : (n + count) * N_TILE]
+                nc.sync.dma_start(out=landed[:], in_=rows.rearrange("(p j) c -> p j c", j=4))
             elif kind in ("mix_a", "mix_b"):
                 g, n = step[1:]
                 if (g, n) not in grouped:
-                    grouped[g, n] = stage.tile([P, N_TILE, 4], BF16, name="grouped", bufs=5, align_bytes=64)
+                    grouped[g, n] = stage.tile([P, N_TILE, 4], BF16, name="grouped", bufs=4, align_bytes=64)
                 split = vector_cols(g, n)
                 cols = slice(0, split) if kind == "mix_b" else slice(split, N_TILE)
                 copy(
@@ -286,11 +308,13 @@ def tile_mtp_combined_projection_g6_kernel(
             elif kind == "drain":
                 n, t = step[1:]
                 nc.vector.tensor_tensor(
-                    out=y_f32[:, n, t, :], in0=banks[n, t][:], in1=bias_rows[:, n * N_TILE : (n + 1) * N_TILE], op=ADD
+                    out=y_f32(n, t, 1), in0=banks[n, t][:], in1=bias_rows[:, n * N_TILE : (n + 1) * N_TILE], op=ADD
                 )
             elif kind == "cast":
                 n, t = step[1:]
-                dst = y_bf16[:, n, t, :].rearrange("p (u q e) -> p u q e", u=2, e=2)
+                count = turn_of["turn", n, t][3]
+                rounded[n, t] = stage.tile([P, 2 * N_TILE], BF16, name="rounded", bufs=5)
+                dst = rounded[n, t][:, : count * N_TILE].rearrange("p (u q e) -> p u q e", u=2, e=2)
                 if (n, t) == (2, 7):
                     nc.vector.tensor_tensor(
                         out=dst,
@@ -299,44 +323,54 @@ def tile_mtp_combined_projection_g6_kernel(
                         op=ADD,
                     )
                 else:
-                    copy(engine, dst, word_order(y_f32[:, n, t, :]))
+                    copy(engine, dst, word_order(y_f32(n, t, count)))
             elif kind == "turn":
                 n, t, count, bank = step[1:]
                 banks["turn", n, t] = bank_tile(bank)
-                for i in range(count):
-                    words = y_bf16[:, n, t + i, :].bitcast(F32)
-                    for u in range(2):
-                        col = (2 * i + u) * P
-                        nc.tensor.transpose(banks["turn", n, t][:, col : col + P], words[:, u * P : (u + 1) * P], identity[:])
+                words = rounded[n, t][:, : count * N_TILE].bitcast(F32)
+                for j in range(2 * count):
+                    cols = slice(j * P, (j + 1) * P)
+                    nc.tensor.transpose(banks["turn", n, t][:, cols], words[:, cols], identity[:])
             elif kind == "gather":
                 n, t = step[1:]
                 count = turn_of["turn", n, t][3]
-                turned[n, t] = stage.tile([P, 2 * P * 4], BF16, name="turned", bufs=4, align_bytes=64)
+                home = (0, t - t % 2) if n == 0 else (2, 0 if t == 2 else t)
+                if home not in turned:
+                    turned[home] = stage.tile([P, 2, 2, 4 * P], BF16, name="turned", bufs=3, align_bytes=64)
+                if n == 0:
+                    dst = turned[home][:, :, t % 2, :]
+                else:
+                    dst = turned[home][:, 1 if t == 2 else 0, :count, :]
                 nc.scalar.copy(
-                    out=turned[n, t][:, : count * 4 * P].bitcast(F32).rearrange("p (i m u) -> p i m u", i=count, u=2),
-                    in_=banks["turn", n, t][:, : count * 2 * P].rearrange("p (i u m) -> p i m u", i=count, u=2),
+                    out=dst.bitcast(F32).rearrange("p b (m u) -> p b m u", u=2),
+                    in_=banks["turn", n, t][:, : count * 2 * P].rearrange("p (u b m) -> p b m u", u=2, b=count),
                 )
             elif kind == "quant_y":
                 n, t = step[1:]
-                count = turn_of["turn", n, t][3]
+                count = quant_tokens(n, t)
                 tokens = slice(t * P, (t + count) * P)
+                flat = turned[(0, t) if n < 2 else (2, t)][:].rearrange("p a b c -> p (a b c)")
+                start = n * 8 * P if n < 2 else 0
                 nc.vector.quantize_mx(
                     out=y_codes[:, n, tokens].bitcast(FP8X4),
                     scales=y_scales[:, n, tokens],
-                    in_=turned[n, t][:, : count * 4 * P],
+                    in_=flat[:, start : start + count * 4 * P],
                 )
             elif kind == "store_y":
-                n, t, count = step[1:]
-                rows = out_0[t * P : (t + count) * P, n * N_TILE : (n + 1) * N_TILE]
-                nc.sync.dma_start(out=rows.rearrange("(i p) f -> p i f", p=P), in_=y_f32[:, n, t : t + count, :])
+                n, t = step[1:]
+                count = 2 if n == 0 else 1
+                nc.sync.dma_start(
+                    out=out_0[t * P : (t + 1) * P, n * N_TILE : (n + count) * N_TILE], in_=y_f32(n, t, count)
+                )
             elif kind == "store_words":
                 n, t, count = step[1:]
                 words = out_1[n].rearrange("p m t -> p (m t)").bitcast(I32)
                 tokens = slice(t * P, (t + count) * P)
                 nc.sync.dma_start(out=words[:, tokens], in_=y_codes[:, n, tokens].bitcast(I32))
             elif kind == "store_scales":
-                first, end, quad = step[1:]
-                rows = out_2[first:end, 4 * quad : 4 * quad + 4, :].rearrange("n r m -> r n m")
+                first, end, t, count, quad = step[1:]
+                tokens = slice(t * P, (t + count) * P)
+                rows = out_2[first:end, 4 * quad : 4 * quad + 4, tokens].rearrange("n r m -> r n m")
                 engines[engine].dma_start(
-                    out=rows.bitcast(I32), in_=y_scales[32 * quad : 32 * quad + 4, first:end, :].bitcast(I32)
+                    out=rows.bitcast(I32), in_=y_scales[32 * quad : 32 * quad + 4, first:end, tokens].bitcast(I32)
                 )

@@ -22,7 +22,7 @@ SWEEPS = 3
 TOKEN_TILES = 8
 HALF = N_TILE // 2
 EARLY_VECTOR_COLS = 336
-TURN_AFTER = [4, 6, 8, 9, 13]
+TURN_AFTER = [6, 10, 14]
 SHARES = {(5, 0): 256, (5, 1): 256}
 
 
@@ -31,7 +31,7 @@ def vector_cols(g, n):
         return SHARES[g, n]
     if n == 0 or (g, n) == (5, 1):
         return EARLY_VECTOR_COLS
-    return 256 if n == 1 else HALF
+    return 224 if n == 1 else HALF
 
 
 def tensor_order():
@@ -39,28 +39,31 @@ def tensor_order():
     order += [("mm", n, t, g, 4 * n + t) for g in range(PASSES) for n in range(2) for t in range(4)]
     tiles = [(n, t) for t in range(4, 8) for n in range(2)] + [(2, t) for t in range(TOKEN_TILES)]
     after = TURN_AFTER
-    runs = [[(0, 0), (0, 1)], [(0, 2), (0, 3)], [(0, 4), (0, 5)], [(0, 6), (0, 7)], [(2, 0), (2, 2)]]
-    for j, (n, t) in enumerate(tiles):
+    runs = [[(0, t) for t in range(4)], [(0, t) for t in range(4, 8)], [(2, 0), (2, 2), (2, 4)]]
+    turns = 0
+    for j, (n, t) in enumerate(tiles[:-1]):
         order += [("mm", n, t, g, j % 4) for g in range(PASSES)]
         if j in after:
-            r = after.index(j)
-            order += [("turn",) + unit + (2, 4 + 2 * (r % 2) + i) for i, unit in enumerate(runs[r])]
-    order += [("turn", 2, 4, 2, 6), ("turn", 2, 6, 1, 7), ("turn", 2, 7, 1, 4)]
+            for unit in runs[after.index(j)]:
+                order.append(("turn",) + unit + (2, 4 + turns % 4))
+                turns += 1
+    order += [("mm", 2, 7, g, bank, half) for half, bank in enumerate((3, 0)) for g in range(PASSES)]
+    order += [("turn", 2, t, 1, 4 + (turns + i) % 4) for i, t in enumerate((6, 7))]
     return order
 
 
 VECTOR_TEXT = """
 b00 b01 q00 q01 b10 b11 q10 q11 b20 b21 q20 q21 b30 b31 q30 q31 b40 b41 q40 b50 q41 q50 b51 q51
 e00 e01 e10 e11 e02 e12 e03 e13
-e04 b02 e14 q02 b12 e05 q12 b22 e15 q22 b32 e06 q32 b42 z00 z10 e16 q42 b52 e07 q52 c05 e17 z02 z12
-e20 z04 z14 e21 z06 z16 e22 e23 e24 e25 c24 z20 e26 c26 c27 e27 z24 z26 z27
+e04 b02 e14 q02 b12 e05 q12 b22 e15 q22 b32 e06 q32 b42 e16 q42 b52 e07 q52 z00 z10 e17 z02 z12
+e20 e21 e22 z04 z14 z06 z16 e23 e24 e25 c24 e26 c26 z20 c270 e270 c271 z24 e271 z26 z27
 """
 SCALAR_TEXT = """
 B a00 a01 a10 a11 a20 a21 a30 a31 a40 a41 a50 a51
-c00 c01 a02 a12 a22 c02 a32 y00 y01 a42 c03 a52 y02 y03 c04 c06 c07 y04 y05 y06 y07 c20 c22 y20 y22 y24 y26 y27 s23082 s23083
+c00 c01 a02 a12 a22 c02 a32 c03 a42 a52 y00 y01 y02 y03 c04 c05 c06 c07 c20 y04 y05 y06 y07 c22 y20 y22 y24 y26 y27 s23082 s23083
 """
 STORE_TEXT = """
-o00 o01 o02 o03 o04 o05 o06 w004 w104 o07 o20 o21 w044 w144 s02080 s02081 s02082 s02083 o22 o23 o24 o25 w204 o26 o27 w242 w262 s23080 s23081
+o00 o01 o02 o03 o04 o05 o06 o07 w004 w104 o20 o21 o22 w044 w144 s02080 s02081 s02082 s02083 o23 o24 o25 o26 w204 w242 o27 w262 s23080 s23081
 """
 KINDS = {"a": "mix_a", "b": "mix_b", "q": "quant_w", "e": "drain", "c": "cast", "y": "gather", "z": "quant_y",
          "o": "store_y", "w": "store_words", "s": "store_scales", "h": "hid_memset", "B": "bias_copy"}
@@ -100,10 +103,12 @@ def quant_starts(n):
 def needs(step, bank_reader, turn_of):
     kind = step[0]
     if kind == "mm":
-        n, t, g, bank = step[1:]
+        n, t, g, bank = step[1:5]
         out = [("quant_w", g, n), ("load_x", g, t // 4)] + [("load_scales", g // 3, quad) for quad in range(4)]
         return out + bank_reader.get(step, [])
     if kind == "turn":
+        if step[1:3] == (2, 7):
+            return [("cast", 2, 7, 0), ("cast", 2, 7, 1)] + bank_reader.get(step, [])
         return [("cast", step[1], step[2])] + bank_reader.get(step, [])
     if kind in ("mix_a", "mix_b"):
         g, n = step[1:]
@@ -111,11 +116,11 @@ def needs(step, bank_reader, turn_of):
     if kind == "quant_w":
         return [("mix_a",) + step[1:], ("mix_b",) + step[1:]]
     if kind == "drain":
-        return [turn_of["close", step[1], step[2]], ("bias_copy",)]
+        return [turn_of[("close",) + step[1:]], ("bias_copy",)]
     if kind == "cast":
-        n, t = step[1:]
+        n, t = step[1:3]
         if (n, t) == (2, 7):
-            return [turn_of["close", 2, 7]]
+            return [turn_of[("close",) + step[1:]]]
         if n == 0:
             return [("drain", 0, t), ("drain", 1, t)]
         return [("drain", 2, t + i) for i in range(turn_of["turn", n, t][3])]
@@ -128,6 +133,8 @@ def needs(step, bank_reader, turn_of):
         return [("gather", 2, 0), ("gather", 2, 2)] if t == 0 else [("gather", 2, t)]
     if kind == "store_y":
         n, t = step[1:]
+        if (n, t) == (2, 7):
+            return [("drain", 2, 7, 0), ("drain", 2, 7, 1)]
         return [("drain", 0, t), ("drain", 1, t)] if n == 0 else [("drain", 2, t)]
     if kind == "store_words":
         n, t, count = step[1:]
@@ -150,12 +157,12 @@ def program():
     last = {6: [("bias_copy",)], 7: [("bias_copy",)]}
     for step in lists["tensor"]:
         if step[0] == "mm":
-            n, t, g, bank = step[1:]
+            n, t, g, bank = step[1:5]
             if g == 0:
                 bank_reader[step] = last.get(bank, [])
                 last[bank] = [("drain", n, t)]
             if g == PASSES - 1:
-                turn_of["close", n, t] = step
+                turn_of[("close", n, t) + step[5:]] = step
         if step[0] == "turn":
             n, t, count, bank = step[1:]
             bank_reader[step] = last.get(bank, [])
@@ -196,16 +203,16 @@ def tile_mtp_combined_projection_g6_kernel(
         identity = keep.tile([P, P], F32)
         bias_quads = keep.tile([P, SWEEPS, 4], BF16)
         bias_rows = keep.tile([P, D], BF16)
-        x_codes = keep.tile([P, PASSES, T], U32, align_bytes=64)
-        emb_planes = keep.tile([P, T], U8, align_bytes=64)
-        hid_planes = keep.tile([P, T], U8, align_bytes=64)
+        x_codes = keep.tile([P, PASSES, T], U32, align_bytes=256)
+        emb_planes = keep.tile([P, T], U8, align_bytes=256)
+        hid_planes = keep.tile([P, T], U8, align_bytes=256)
         x_planes = (emb_planes, hid_planes)
-        w_codes = keep.tile([P, SWEEPS, PASSES, N_TILE], U32, align_bytes=64)
-        w_scales = keep.tile([P, SWEEPS, PASSES, N_TILE], U8, align_bytes=64)
+        w_codes = keep.tile([P, SWEEPS, PASSES, N_TILE], U32, align_bytes=256)
+        w_scales = keep.tile([P, SWEEPS, PASSES, N_TILE], U8, align_bytes=256)
         y_wide = keep.tile([P, TOKEN_TILES, 2 * N_TILE], F32)
         y_last = keep.tile([P, TOKEN_TILES * N_TILE], F32)
-        y_codes = keep.tile([P, SWEEPS, T], U32, align_bytes=64)
-        y_scales = keep.tile([P, SWEEPS, T], U8, align_bytes=64)
+        y_codes = keep.tile([P, SWEEPS, T], U32, align_bytes=256)
+        y_scales = keep.tile([P, SWEEPS, T], U8, align_bytes=256)
 
         raw, grouped, banks, rounded, turned = {}, {}, {}, {}, {}
 
@@ -222,6 +229,9 @@ def tile_mtp_combined_projection_g6_kernel(
 
         def bank_tile(bank):
             return psum.tile([P, N_TILE], F32, name="bank%d" % bank)
+
+        def unit_cols(unit):
+            return slice(unit[2] * HALF, (unit[2] + 1) * HALF) if len(unit) == 3 else slice(0, N_TILE)
 
         def word_order(ap):
             return ap.rearrange("p (q u e) -> p u q e", u=2, e=2)
@@ -275,7 +285,7 @@ def tile_mtp_combined_projection_g6_kernel(
             elif kind in ("mix_a", "mix_b"):
                 g, n = step[1:]
                 if (g, n) not in grouped:
-                    grouped[g, n] = stage.tile([P, N_TILE, 4], BF16, name="grouped", bufs=4, align_bytes=64)
+                    grouped[g, n] = stage.tile([P, N_TILE, 4], BF16, name="grouped", bufs=4, align_bytes=256)
                 split = vector_cols(g, n)
                 cols = slice(0, split) if kind == "mix_b" else slice(split, N_TILE)
                 copy(
@@ -291,35 +301,45 @@ def tile_mtp_combined_projection_g6_kernel(
                     in_=grouped[g, n][:].rearrange("p c j -> p (c j)"),
                 )
             elif kind == "mm":
-                n, t, g, bank = step[1:]
+                n, t, g, bank = step[1:5]
+                unit = (n, t) + step[5:]
                 if g == 0:
-                    banks[n, t] = bank_tile(bank)
+                    banks[unit] = bank_tile(bank)
                 side, group = divmod(g, 3)
                 tokens = slice(t * P, (t + 1) * P)
+                cols = unit_cols(unit)
                 nc.tensor.matmul_mx(
-                    out=banks[n, t][:],
+                    out=banks[unit][:, : cols.stop - cols.start],
                     lhsT=x_codes[:, g, tokens].bitcast(FP8X4),
                     lhsT_scale=x_planes[side][4 * group :, tokens],
-                    rhs=w_codes[:, n, g, :].bitcast(FP8X4),
-                    rhs_scale=w_scales[:, n, g, :],
+                    rhs=w_codes[:, n, g, cols].bitcast(FP8X4),
+                    rhs_scale=w_scales[:, n, g, cols],
                     start=(g == 0),
                     stop=(g == PASSES - 1),
                 )
             elif kind == "drain":
-                n, t = step[1:]
+                unit = step[1:]
+                n, t = unit[:2]
+                cols = unit_cols(unit)
                 nc.vector.tensor_tensor(
-                    out=y_f32(n, t, 1), in0=banks[n, t][:], in1=bias_rows[:, n * N_TILE : (n + 1) * N_TILE], op=ADD
+                    out=y_f32(n, t, 1)[:, cols],
+                    in0=banks[unit][:, : cols.stop - cols.start],
+                    in1=bias_rows[:, n * N_TILE : (n + 1) * N_TILE][:, cols],
+                    op=ADD,
                 )
             elif kind == "cast":
-                n, t = step[1:]
+                unit = step[1:]
+                n, t = unit[:2]
                 count = turn_of["turn", n, t][3]
-                rounded[n, t] = stage.tile([P, 2 * N_TILE], BF16, name="rounded", bufs=5)
+                if (n, t) not in rounded:
+                    rounded[n, t] = stage.tile([P, 2 * N_TILE], BF16, name="rounded", bufs=6)
                 dst = rounded[n, t][:, : count * N_TILE].rearrange("p (u q e) -> p u q e", u=2, e=2)
                 if (n, t) == (2, 7):
+                    cols = unit_cols(unit)
                     nc.vector.tensor_tensor(
-                        out=dst,
-                        in0=word_order(banks[n, t][:]),
-                        in1=word_order(bias_rows[:, n * N_TILE : (n + 1) * N_TILE]),
+                        out=dst[:, :, cols.start // 4 : cols.stop // 4, :],
+                        in0=word_order(banks[unit][:, :HALF]),
+                        in1=word_order(bias_rows[:, n * N_TILE : (n + 1) * N_TILE][:, cols]),
                         op=ADD,
                     )
                 else:
@@ -336,7 +356,7 @@ def tile_mtp_combined_projection_g6_kernel(
                 count = turn_of["turn", n, t][3]
                 home = (0, t - t % 2) if n == 0 else (2, 0 if t == 2 else t)
                 if home not in turned:
-                    turned[home] = stage.tile([P, 2, 2, 4 * P], BF16, name="turned", bufs=3, align_bytes=64)
+                    turned[home] = stage.tile([P, 2, 2, 4 * P], BF16, name="turned", bufs=3, align_bytes=256)
                 if n == 0:
                     dst = turned[home][:, :, t % 2, :]
                 else:

from contextlib import ExitStack

import concourse.mybir as mybir
from concourse.masks import make_identity

T, D = 1024, 1536
FLOPS = 2 * T * 2 * D * D

F32 = mybir.dt.float32
BF16 = mybir.dt.bfloat16
I32 = mybir.dt.int32
U32 = mybir.dt.uint32
U8 = mybir.dt.uint8
FP8X4 = mybir.dt.float8_e4m3fn_x4
ADD = mybir.AluOpType.add

P = 128
K_PASS = 512
N_TILE = 512
PASSES = 6
SWEEPS = 3
TOKEN_TILES = 8
HALF = N_TILE // 2
EARLY_VECTOR_COLS = 336
TURN_AFTER = [6, 10, 14]
SHARES = {(5, 0): 256, (5, 1): 256}


def vector_cols(g, n):
    if (g, n) in SHARES:
        return SHARES[g, n]
    if n == 0 or (g, n) == (5, 1):
        return EARLY_VECTOR_COLS
    return 224 if n == 1 else HALF


def tensor_order():
    order = [("bias_turn",)]
    order += [("mm", n, t, g, 4 * n + t) for g in range(PASSES) for n in range(2) for t in range(4)]
    tiles = [(n, t) for t in range(4, 8) for n in range(2)] + [(2, t) for t in range(TOKEN_TILES)]
    after = TURN_AFTER
    runs = [[(0, t) for t in range(4)], [(0, t) for t in range(4, 8)], [(2, 0), (2, 2), (2, 4)]]
    turns = 0
    for j, (n, t) in enumerate(tiles[:-1]):
        order += [("mm", n, t, g, j % 4) for g in range(PASSES)]
        if j in after:
            for unit in runs[after.index(j)]:
                order.append(("turn",) + unit + (2, 4 + turns % 4))
                turns += 1
    order += [("mm", 2, 7, g, bank, half) for half, bank in enumerate((3, 0)) for g in range(PASSES)]
    order += [("turn", 2, t, 1, 4 + (turns + i) % 4) for i, t in enumerate((6, 7))]
    return order


VECTOR_TEXT = """
b00 b01 q00 q01 b10 b11 q10 q11 b20 b21 q20 q21 b30 b31 q30 q31 b40 b41 q40 b50 q41 q50 b51 q51
e00 e01 e10 e11 e02 e12 e03 e13
e04 b02 e14 q02 b12 e05 q12 b22 e15 q22 b32 e06 q32 b42 e16 q42 b52 e07 q52 z00 z10 e17 z02 z12
e20 e21 e22 z04 z14 z06 z16 e23 e24 e25 c24 e26 c26 z20 c270 e270 c271 z24 e271 z26 z27
"""
SCALAR_TEXT = """
B a00 a01 a10 a11 a20 a21 a30 a31 a40 a41 a50 a51
c00 c01 a02 a12 a22 c02 a32 c03 a42 a52 y00 y01 y02 y03 c04 c05 c06 c07 c20 y04 y05 y06 y07 c22 y20 y22 y24 y26 y27 s23082 s23083
"""
STORE_TEXT = """
o00 o01 o02 o03 o04 o05 o06 o07 w004 w104 o20 o21 o22 w044 w144 s02080 s02081 s02082 s02083 o23 o24 o25 o26 w204 w242 o27 w262 s23080 s23081
"""
KINDS = {"a": "mix_a", "b": "mix_b", "q": "quant_w", "e": "drain", "c": "cast", "y": "gather", "z": "quant_y",
         "o": "store_y", "w": "store_words", "s": "store_scales", "h": "hid_memset", "B": "bias_copy"}


def parse(text):
    return [(KINDS[word[0]],) + tuple(int(c) for c in word[1:]) for word in text.split()]


def load_order():
    order = []
    for g in range(PASSES - 1):
        order += [("load_w", g, 0, 2), ("load_x", g, 0)]
    order += [("load_w", 5, 0, 1), ("load_w", 5, 1, 1), ("load_x", 5, 0)]
    order += [("load_x", g, 1) for g in range(PASSES)] + [("load_w", g, 2, 1) for g in range(PASSES)]
    return order


def queues():
    return {
        "tensor": tensor_order(),
        "vector": [("emb_memset",), ("hid_memset",)] + parse(VECTOR_TEXT),
        "scalar": [("load_bias",)] + [("load_scales", 0, quad) for quad in range(4)] + parse(SCALAR_TEXT),
        "sync": load_order() + parse(STORE_TEXT),
        "gpsimd": [("identity",)] + [("load_scales", 1, quad) for quad in range(4)],
    }


def quant_tokens(n, t):
    return {(2, 0): 4, (2, 6): 1, (2, 7): 1}.get((n, t), 2)


def quant_starts(n):
    return (0, 4, 6, 7) if n == 2 else (0, 2, 4, 6)


def needs(step, bank_reader, turn_of):
    kind = step[0]
    if kind == "mm":
        n, t, g, bank = step[1:5]
        out = [("quant_w", g, n), ("load_x", g, t // 4)] + [("load_scales", g // 3, quad) for quad in range(4)]
        return out + bank_reader.get(step, [])
    if kind == "turn":
        if step[1:3] == (2, 7):
            return [("cast", 2, 7, 0), ("cast", 2, 7, 1)] + bank_reader.get(step, [])
        return [("cast", step[1], step[2])] + bank_reader.get(step, [])
    if kind in ("mix_a", "mix_b"):
        g, n = step[1:]
        return [("load_w", g, 0, 2)] if n < 2 and g < 5 else [("load_w", g, n, 1)]
    if kind == "quant_w":
        return [("mix_a",) + step[1:], ("mix_b",) + step[1:]]
    if kind == "drain":
        return [turn_of[("close",) + step[1:]], ("bias_copy",)]
    if kind == "cast":
        n, t = step[1:3]
        if (n, t) == (2, 7):
            return [turn_of[("close",) + step[1:]]]
        if n == 0:
            return [("drain", 0, t), ("drain", 1, t)]
        return [("drain", 2, t + i) for i in range(turn_of["turn", n, t][3])]
    if kind == "gather":
        return [turn_of["turn", step[1], step[2]]]
    if kind == "quant_y":
        n, t = step[1:]
        if n < 2:
            return [("gather", 0, t), ("gather", 0, t + 1)]
        return [("gather", 2, 0), ("gather", 2, 2)] if t == 0 else [("gather", 2, t)]
    if kind == "store_y":
        n, t = step[1:]
        if (n, t) == (2, 7):
            return [("drain", 2, 7, 0), ("drain", 2, 7, 1)]
        return [("drain", 0, t), ("drain", 1, t)] if n == 0 else [("drain", 2, t)]
    if kind == "store_words":
        n, t, count = step[1:]
        return [("quant_y", n, s) for s in quant_starts(n) if t <= s < t + count]
    if kind == "store_scales":
        first, end, t, count, quad = step[1:]
        return [("quant_y", n, s) for n in range(first, end) for s in quant_starts(n) if t <= s < t + count]
    if kind == "load_scales":
        return [("emb_memset",)] if step[1] == 0 else [("hid_memset",)]
    if kind == "bias_turn":
        return [("identity",), ("load_bias",)]
    if kind == "bias_copy":
        return [("bias_turn",)]
    return []


def program():
    lists = queues()
    bank_reader, turn_of = {}, {}
    last = {6: [("bias_copy",)], 7: [("bias_copy",)]}
    for step in lists["tensor"]:
        if step[0] == "mm":
            n, t, g, bank = step[1:5]
            if g == 0:
                bank_reader[step] = last.get(bank, [])
                last[bank] = [("drain", n, t)]
            if g == PASSES - 1:
                turn_of[("close", n, t) + step[5:]] = step
        if step[0] == "turn":
            n, t, count, bank = step[1:]
            bank_reader[step] = last.get(bank, [])
            last[bank] = [("gather", n, t)]
            turn_of["turn", n, t] = step
    text, written = [], set()
    place = {engine: 0 for engine in lists}
    total = sum(len(steps) for steps in lists.values())
    while len(text) < total:
        before = len(text)
        for engine, steps in lists.items():
            if place[engine] < len(steps):
                step = steps[place[engine]]
                wanted = needs(step, bank_reader, turn_of)
                if all(w in written for w in wanted):
                    text.append((engine, step, wanted))
                    written.add(step)
                    place[engine] += 1
        assert len(text) > before
    return text, turn_of


def tile_mtp_combined_projection_g6_kernel(
    tc, emb_words, emb_scales, hid_words, hid_scales, w_emb, w_hid, bias, out_0, out_1, out_2
):
    nc = tc.nc
    engines = {"scalar": nc.scalar, "sync": nc.sync, "gpsimd": nc.gpsimd}
    weights = (w_emb, w_hid)
    x_words = (emb_words, hid_words)
    x_scale_rows = (emb_scales, hid_scales)

    with ExitStack() as ctx:
        keep = ctx.enter_context(tc.tile_pool(name="keep", bufs=1))
        stage = ctx.enter_context(tc.tile_pool(name="stage", bufs=1))
        psum = ctx.enter_context(tc.psum_pool(name="psum", bufs=1))
        ctx.enter_context(tc.manual_schedule())

        identity = keep.tile([P, P], F32)
        bias_quads = keep.tile([P, SWEEPS, 4], BF16)
        bias_rows = keep.tile([P, D], BF16)
        x_codes = keep.tile([P, PASSES, T], U32, align_bytes=256)
        emb_planes = keep.tile([P, T], U8, align_bytes=256)
        hid_planes = keep.tile([P, T], U8, align_bytes=256)
        x_planes = (emb_planes, hid_planes)
        w_codes = keep.tile([P, SWEEPS, PASSES, N_TILE], U32, align_bytes=256)
        w_scales = keep.tile([P, SWEEPS, PASSES, N_TILE], U8, align_bytes=256)
        y_wide = keep.tile([P, TOKEN_TILES, 2 * N_TILE], F32)
        y_last = keep.tile([P, TOKEN_TILES * N_TILE], F32)
        y_codes = keep.tile([P, SWEEPS, T], U32, align_bytes=256)
        y_scales = keep.tile([P, SWEEPS, T], U8, align_bytes=256)

        raw, grouped, banks, rounded, turned = {}, {}, {}, {}, {}

        def y_f32(n, t, count):
            if n < 2:
                return y_wide[:, t, n * N_TILE : (n + count) * N_TILE]
            return y_last[:, t * N_TILE : (t + count) * N_TILE]

        def copy(engine, out, in_):
            if engine == "vector":
                nc.vector.tensor_copy(out=out, in_=in_)
            else:
                nc.scalar.copy(out=out, in_=in_)

        def bank_tile(bank):
            return psum.tile([P, N_TILE], F32, name="bank%d" % bank)

        def unit_cols(unit):
            return slice(unit[2] * HALF, (unit[2] + 1) * HALF) if len(unit) == 3 else slice(0, N_TILE)

        def word_order(ap):
            return ap.rearrange("p (q u e) -> p u q e", u=2, e=2)

        text, turn_of = program()
        for engine, step, wanted in text:
            kind = step[0]
            if kind == "identity":
                make_identity(nc, identity[:])
            elif kind == "load_bias":
                nc.scalar.dma_start(out=bias_quads[:], in_=bias.rearrange("(n p c) -> p n c", n=SWEEPS, c=4))
            elif kind == "bias_turn":
                words = bias_quads[:].rearrange("p n c -> p (n c)").bitcast(F32)
                banks["bias"] = (bank_tile(6), bank_tile(7))
                for j in range(2 * SWEEPS):
                    nc.tensor.transpose(
                        banks["bias"][j // 4][:, (j % 4) * P : (j % 4 + 1) * P],
                        words[:, j : j + 1].to_broadcast([P, P]),
                        identity[:],
                    )
            elif kind == "bias_copy":
                for n in range(SWEEPS):
                    src = banks["bias"][n // 2][:, (n % 2) * 2 * P : (n % 2 + 1) * 2 * P]
                    dst = bias_rows[:, n * N_TILE : (n + 1) * N_TILE].bitcast(F32)
                    nc.scalar.copy(out=dst.rearrange("p (q u) -> p q u", u=2), in_=src.rearrange("p (u q) -> p q u", u=2))
            elif kind in ("emb_memset", "hid_memset"):
                nc.vector.memset(x_planes[kind == "hid_memset"][:].bitcast(I32), 0)
            elif kind == "load_scales":
                side, quad = step[1:]
                engines[engine].dma_start(
                    out=x_planes[side][32 * quad : 32 * quad + 12, :].bitcast(I32),
                    in_=x_scale_rows[side][:, 4 * quad : 4 * quad + 4, :].bitcast(I32),
                )
            elif kind == "load_x":
                g, half = step[1:]
                side, group = divmod(g, 3)
                tokens = slice(half * T // 2, (half + 1) * T // 2)
                words = x_words[side][group].rearrange("p m t -> p (m t)").bitcast(I32)
                nc.sync.dma_start(out=x_codes[:, g, tokens].bitcast(I32), in_=words[:, tokens])
            elif kind == "load_w":
                g, n, count = step[1:]
                side, group = divmod(g, 3)
                if count == 2:
                    landed = stage.tile([P, 4, 2 * N_TILE], BF16, name="raw_wide", bufs=3)
                else:
                    landed = stage.tile([P, 4, N_TILE], BF16, name="raw_narrow", bufs=6)
                for i in range(count):
                    raw[g, n + i] = landed[:, :, i * N_TILE : (i + 1) * N_TILE]
                rows = weights[side][group * K_PASS : (group + 1) * K_PASS, n * N_TILE : (n + count) * N_TILE]
                nc.sync.dma_start(out=landed[:], in_=rows.rearrange("(p j) c -> p j c", j=4))
            elif kind in ("mix_a", "mix_b"):
                g, n = step[1:]
                if (g, n) not in grouped:
                    grouped[g, n] = stage.tile([P, N_TILE, 4], BF16, name="grouped", bufs=4, align_bytes=256)
                split = vector_cols(g, n)
                cols = slice(0, split) if kind == "mix_b" else slice(split, N_TILE)
                copy(
                    engine,
                    grouped[g, n][:, cols, :].rearrange("p (c i) j -> p c j i", i=4),
                    raw[g, n][:, :, cols].rearrange("p j (c i) -> p c j i", i=4),
                )
            elif kind == "quant_w":
                g, n = step[1:]
                nc.vector.quantize_mx(
                    out=w_codes[:, n, g, :].bitcast(FP8X4),
                    scales=w_scales[:, n, g, :],
                    in_=grouped[g, n][:].rearrange("p c j -> p (c j)"),
                )
            elif kind == "mm":
                n, t, g, bank = step[1:5]
                unit = (n, t) + step[5:]
                if g == 0:
                    banks[unit] = bank_tile(bank)
                side, group = divmod(g, 3)
                tokens = slice(t * P, (t + 1) * P)
                cols = unit_cols(unit)
                nc.tensor.matmul_mx(
                    out=banks[unit][:, : cols.stop - cols.start],
                    lhsT=x_codes[:, g, tokens].bitcast(FP8X4),
                    lhsT_scale=x_planes[side][4 * group :, tokens],
                    rhs=w_codes[:, n, g, cols].bitcast(FP8X4),
                    rhs_scale=w_scales[:, n, g, cols],
                    start=(g == 0),
                    stop=(g == PASSES - 1),
                )
            elif kind == "drain":
                unit = step[1:]
                n, t = unit[:2]
                cols = unit_cols(unit)
                nc.vector.tensor_tensor(
                    out=y_f32(n, t, 1)[:, cols],
                    in0=banks[unit][:, : cols.stop - cols.start],
                    in1=bias_rows[:, n * N_TILE : (n + 1) * N_TILE][:, cols],
                    op=ADD,
                )
            elif kind == "cast":
                unit = step[1:]
                n, t = unit[:2]
                count = turn_of["turn", n, t][3]
                if (n, t) not in rounded:
                    rounded[n, t] = stage.tile([P, 2 * N_TILE], BF16, name="rounded", bufs=6)
                dst = rounded[n, t][:, : count * N_TILE].rearrange("p (u q e) -> p u q e", u=2, e=2)
                if (n, t) == (2, 7):
                    cols = unit_cols(unit)
                    nc.vector.tensor_tensor(
                        out=dst[:, :, cols.start // 4 : cols.stop // 4, :],
                        in0=word_order(banks[unit][:, :HALF]),
                        in1=word_order(bias_rows[:, n * N_TILE : (n + 1) * N_TILE][:, cols]),
                        op=ADD,
                    )
                else:
                    copy(engine, dst, word_order(y_f32(n, t, count)))
            elif kind == "turn":
                n, t, count, bank = step[1:]
                banks["turn", n, t] = bank_tile(bank)
                words = rounded[n, t][:, : count * N_TILE].bitcast(F32)
                for j in range(2 * count):
                    cols = slice(j * P, (j + 1) * P)
                    nc.tensor.transpose(banks["turn", n, t][:, cols], words[:, cols], identity[:])
            elif kind == "gather":
                n, t = step[1:]
                count = turn_of["turn", n, t][3]
                home = (0, t - t % 2) if n == 0 else (2, 0 if t == 2 else t)
                if home not in turned:
                    turned[home] = stage.tile([P, 2, 2, 4 * P], BF16, name="turned", bufs=3, align_bytes=256)
                if n == 0:
                    dst = turned[home][:, :, t % 2, :]
                else:
                    dst = turned[home][:, 1 if t == 2 else 0, :count, :]
                nc.scalar.copy(
                    out=dst.bitcast(F32).rearrange("p b (m u) -> p b m u", u=2),
                    in_=banks["turn", n, t][:, : count * 2 * P].rearrange("p (u b m) -> p b m u", u=2, b=count),
                )
            elif kind == "quant_y":
                n, t = step[1:]
                count = quant_tokens(n, t)
                tokens = slice(t * P, (t + count) * P)
                flat = turned[(0, t) if n < 2 else (2, t)][:].rearrange("p a b c -> p (a b c)")
                start = n * 8 * P if n < 2 else 0
                nc.vector.quantize_mx(
                    out=y_codes[:, n, tokens].bitcast(FP8X4),
                    scales=y_scales[:, n, tokens],
                    in_=flat[:, start : start + count * 4 * P],
                )
            elif kind == "store_y":
                n, t = step[1:]
                count = 2 if n == 0 else 1
                nc.sync.dma_start(
                    out=out_0[t * P : (t + 1) * P, n * N_TILE : (n + count) * N_TILE], in_=y_f32(n, t, count)
                )
            elif kind == "store_words":
                n, t, count = step[1:]
                words = out_1[n].rearrange("p m t -> p (m t)").bitcast(I32)
                tokens = slice(t * P, (t + count) * P)
                nc.sync.dma_start(out=words[:, tokens], in_=y_codes[:, n, tokens].bitcast(I32))
            elif kind == "store_scales":
                first, end, t, count, quad = step[1:]
                tokens = slice(t * P, (t + count) * P)
                rows = out_2[first:end, 4 * quad : 4 * quad + 4, tokens].rearrange("n r m -> r n m")
                engines[engine].dma_start(
                    out=rows.bitcast(I32), in_=y_scales[32 * quad : 32 * quad + 4, first:end, tokens].bitcast(I32)
                )
